import numpy as np, ml_dtypes
CORES = [83,85,87,115,117,119]
N = 6
import mx_ref
NC, G = 512, 4
C = np.float32(0.029)
CNT = [[0,0,272,80,0,160],[80,272,32,0,16,112],[0,16,112,256,128,0],[32,112,0,144,144,80],[272,112,0,0,112,16],[128,0,96,32,112,144]]
OFF = [[sum(c[:e]) for e in range(N + 1)] for c in CNT]
BF = ml_dtypes.bfloat16
def cut(t, i, w=512):
    return t[:, w * i:w * i + w]
def tile(rs):
    return np.stack(rs, axis=2).reshape(128, -1).astype(BF)
def layer(w, X):
    out = []
    for i in range(G):
        for t in range(len(X)):
            p = mx_ref.matmul(mx_ref.quantize(cut(w, len(X) * i + t)), X[t])
            z = p if t == 0 else z + p
        out.append(z)
    return out
def act(Z):
    return [np.maximum(z, 0) * C for z in Z]
def setup_inputs(rng):
    def f(*shape):
        return mx_ref.flush((rng.standard_normal(shape, dtype=np.float32) * np.exp2(rng.integers(-2, 3, shape[:-1] + (1,)))).astype(BF))
    return {"x": f(N, 128, 4 * NC), "w1": f(N, 128, G * 512), "w2": f(N, 128, 512)}
def setup_inputs_blocks(rng):
    d = setup_inputs(rng)
    for k in ("x", "w1", "w2"): d[k] = mx_ref.spread(d[k], rng, 4)
    return d
def setup_inputs_wide(rng):
    d = setup_inputs(rng)
    for k in ("x", "w1", "w2"): d[k] = mx_ref.flush((d[k].astype(np.float32) * np.exp2(rng.integers(-8, 9, (N, 1, 1))).astype(np.float32)).astype(BF))
    return d
def setup_inputs_zeros(rng):
    d = setup_inputs(rng); v = d["x"].reshape(N, 128, -1, 4).copy()
    v[np.broadcast_to((rng.random((N, 1, v.shape[2], 1)) < 0.33), v.shape)] = 0
    d["x"] = v.reshape(d["x"].shape)
    return d
def reference(x, w1, w2):
    y = np.zeros((N, 128, NC), np.float32)
    for e in range(N):
        t = np.concatenate([x[j][:, 4 * OFF[j][e]:4 * OFF[j][e + 1]] for j in range(N)], axis=1)
        p = mx_ref.matmul(mx_ref.quantize(w2[e]), mx_ref.quantize(tile(act(layer(w1[e], [mx_ref.quantize(t)])))))
        c = 0
        for j in range(N):
            a, b = OFF[j][e], OFF[j][e + 1]
            y[j][:, a:b] = p[:, c:c + b - a]; c += b - a
    return {"y": y}

@@ -1,0 +1,269 @@
+from concourse.bass import DstId, RemoteDMATransfer
+from concourse.mybir import dt, AluOpType, ActivationFunctionType
+
+NC = 512
+TW = 128
+G = 4
+SLOT = (G + 1) * TW
+PER_CHIP = 3
+CONST = 0.029
+BANK = 512
+
+SCRATCH = {
+    "xt": ("sbuf", [128, 4 * NC], "bfloat16"),
+    "w1t": ("sbuf", [128, 4 * G * TW], "bfloat16"),
+    "w2t": ("sbuf", [128, 4 * TW], "bfloat16"),
+    "xq": ("sbuf", [128, NC], "float8_e4m3fn_x4"),
+    "xs": ("sbuf", [128, NC], "uint8"),
+    "rq": ("sbuf", [128, NC], "float8_e4m3fn_x4"),
+    "rs": ("sbuf", [128, NC], "uint8"),
+    "wq": ("sbuf", [128, PER_CHIP * SLOT], "float8_e4m3fn_x4"),
+    "ws": ("sbuf", [128, PER_CHIP * SLOT], "uint8"),
+    "hx": ("sbuf", [128, 4 * NC], "bfloat16"),
+    "hl": ("sbuf", [128, 4 * NC], "bfloat16"),
+    "hxq": ("sbuf", [128, NC], "float8_e4m3fn_x4"),
+    "hxs": ("sbuf", [128, NC], "uint8"),
+    "hlq": ("sbuf", [128, NC], "float8_e4m3fn_x4"),
+    "hls": ("sbuf", [128, NC], "uint8"),
+    "px": ("sbuf", [128, NC], "float32"),
+    "yl": ("sbuf", [128, NC], "float32"),
+    "yr": ("sbuf", [128, NC], "float32"),
+    "ps": ("psum", [128, 8 * BANK], "float32"),
+}
+SEMAPHORES = (["ld_xc", "ld_xl", "ld_w1", "ld_w2", "q_xc", "q_xl", "q_w1", "q_w2", "tok", "hq_x", "hq_l", "pc_x", "pc_l",
+               "ret", "sent", "st"]
+              + ["wa%d" % k for k in range(PER_CHIP)] + ["zb%d" % b for b in range(8)] + ["a%d" % s for s in range(2 * PER_CHIP)])
+
+
+def _perms(a):
+    if len(a) <= 1:
+        return [list(a)]
+    out = []
+    for i in range(len(a)):
+        for p in _perms(a[:i] + a[i + 1:]):
+            out.append([a[i]] + p)
+    return out
+
+
+def _window(cnt_row, off_row, experts):
+    assert experts == list(range(experts[0], experts[-1] + 1))
+    base = off_row[experts[0]]
+    width = off_row[experts[-1] + 1] - base
+    assert TW <= width <= NC
+    runs = []
+    for e in experts:
+        c = cnt_row[e]
+        if c:
+            pos = off_row[e] - base
+            n = max(c, TW)
+            runs.append({"e": e, "cnt": c, "pos": pos, "a": min(pos, width - n), "n": n})
+    return {"base": base, "W": width, "runs": runs}
+
+
+def _plan(T, topo):
+    cnt = T.tables["CNT"]
+    n = len(T.cores)
+    off = [[sum(row[:e]) for e in range(n + 1)] for row in cnt]
+    chip = [topo.chip(c) for c in T.cores]
+    home = [[k for k in range(n) if chip[k] == chip[j]] for j in range(n)]
+    away = [[k for k in range(n) if chip[k] != chip[j]] for j in range(n)]
+    loc = [_window(cnt[j], off[j], home[j]) for j in range(n)]
+    crs = [_window(cnt[j], off[j], away[j]) for j in range(n)]
+    worker = {}
+    for ch in sorted(set(chip)):
+        workers = [k for k in range(n) if chip[k] == ch]
+        clients = [k for k in range(n) if chip[k] != ch]
+        best = None
+        for p in _perms(clients):
+            if any(sum(s["n"] for s in loc[w]["runs"] + crs[c]["runs"]) < NC for w, c in zip(workers, p)):
+                continue
+            port = {}
+            for w, c in zip(workers, p):
+                d = topo.die(T.cores[w])
+                port[d] = port.get(d, 0) + crs[c]["W"]
+            key = (max(port.values()), sorted((loc[w]["W"] + crs[c]["W"] for w, c in zip(workers, p)), reverse=True))
+            if best is None or key < best[0]:
+                best = (key, p)
+        for w, c in zip(workers, best[1]):
+            worker[c] = w
+    client = {w: c for c, w in worker.items()}
+    need = [set(s["e"] for s in loc[k]["runs"] + crs[client[k]]["runs"]) for k in range(n)]
+    return {"home": home, "loc": loc, "crs": crs, "worker": worker, "client": client, "need": need}
+
+
+def _engines(mask):
+    return bin(mask).count("1")
+
+
+def rank_program(g, core, T, topo):
+    r = T.rank_of(core)
+    if r is None:
+        return
+    P = _plan(T, topo)
+    S = T.sem
+    tq, vq, sq, yq = g.tensor, g.vector, g.scalar, g.sync
+    u8 = dt.uint8
+    mates = P["home"][r]
+    slot = {e: k for k, e in enumerate(mates)}
+    loc, crs = P["loc"][r], P["crs"][r]
+    client, server = P["client"][r], P["worker"][r]
+    cwin = P["crs"][client]
+    xa, xb = crs["base"], crs["base"] + crs["W"]
+    la, lb = loc["base"], loc["base"] + loc["W"]
+    base = slot[r] * SLOT
+
+    seen = {}
+
+    def wait(q, name, val):
+        k = (q is tq, q is vq, q is sq, q is yq, name)
+        if seen.get(k, 0) < val:
+            seen[k] = val
+            q.wait_ge(S[name], val)
+
+    yq.dma_start(T.xt[:, 4 * xa:4 * xb], T.x[:, 4 * xa:4 * xb]).then_inc(S.ld_xc, 16)
+    sq.dma_start(T.w1t[:], T.w1[:]).then_inc(S.ld_w1, 16)
+    sq.dma_start(T.w2t[:], T.w2[:]).then_inc(S.ld_w2, 16)
+    yq.dma_start(T.xt[:, 4 * la:4 * lb], T.x[:, 4 * la:4 * lb]).then_inc(S.ld_xl, 16)
+
+    wait(vq, "ld_xc", 16)
+    vq.quantize_mx(T.xq[:, xa:xb], T.xs[:, xa:xb], T.xt[:, 4 * xa:4 * xb]).then_inc(S.q_xc, 1)
+    wait(vq, "ld_w1", 16)
+    vq.quantize_mx(T.wq[:, base:base + G * TW], T.ws[:, base:base + G * TW], T.w1t[:]).then_inc(S.q_w1, 1)
+    wait(vq, "ld_w2", 16)
+    vq.quantize_mx(T.wq[:, base + G * TW:base + SLOT], T.ws[:, base + G * TW:base + SLOT], T.w2t[:]).then_inc(S.q_w2, 1)
+    wait(vq, "ld_xl", 16)
+    vq.quantize_mx(T.xq[:, la:lb], T.xs[:, la:lb], T.xt[:, 4 * la:4 * lb]).then_inc(S.q_xl, 1)
+
+    sent = 0
+    dst = T.cores[server]
+    assert topo.may_write(core, dst)
+    rid, pid, _ = topo.addr(dst)
+    m = topo.mask(core, dst)
+    g.wait_ge(S.q_xc, 1)
+    g.remote_dma(T.rq[:, 0:crs["W"]].bitcast(u8), T.xq[:, xa:xb].bitcast(u8), S.tok, S.sent, pid, rid, m)
+    g.remote_dma(T.rs[:, 0:crs["W"]], T.xs[:, xa:xb], S.tok, S.sent, pid, rid, m)
+    sent += 2 * _engines(m)
+
+    takers = [k for k in mates if k != r and r in P["need"][k]]
+    if takers:
+        m = topo.mask(core, T.cores[takers[0]])
+        ids = []
+        for k in takers:
+            assert topo.may_write(core, T.cores[k])
+            m &= topo.mask(core, T.cores[k])
+            rid, pid, _ = topo.addr(T.cores[k])
+            ids.append(DstId(rid=rid, pnc=pid))
+        g.wait_ge(S.q_w1, 1)
+        g.wait_ge(S.q_w2, 1)
+        for ap in (T.wq[:, base:base + SLOT].bitcast(u8), T.ws[:, base:base + SLOT]):
+            g.remote_dma_fused([RemoteDMATransfer(dst_ids=ids, dma_engine_mask=m, remote_sem=S["wa%d" % slot[r]],
+                                                  srcs=[ap], dsts=[ap for _ in takers])], local_sem=S.sent)
+            sent += _engines(m)
+
+    def w_arrival(e):
+        src = T.cores[e]
+        mm = topo.mask(src, core)
+        for k in P["home"][e]:
+            if k != e and e in P["need"][k]:
+                mm &= topo.mask(src, T.cores[k])
+        return "wa%d" % slot[e], 2 * _engines(mm)
+
+    tok_total = 2 * _engines(topo.mask(T.cores[client], core))
+
+    written = [0] * 8
+    release = [None] * 8
+    jobs = [0]
+    nseg = [0]
+
+    def layer1(run, away_side):
+        k = jobs[0]
+        jobs[0] += 1
+        sem_a = "a%d" % nseg[0]
+        nseg[0] += 1
+        run["sem"] = sem_a
+        e, n, a = run["e"], run["n"], run["a"]
+        if away_side:
+            wait(tq, "tok", tok_total)
+            rhs, rhs_s, h = T.rq[:, a:a + n], T.rs[:, a:a + n], T.hx
+        else:
+            wait(tq, "q_xl", 1)
+            rhs, rhs_s, h = T.xq[:, la + a:la + a + n], T.xs[:, la + a:la + a + n], T.hl
+        if e == r:
+            wait(tq, "q_w1", 1)
+        else:
+            wait(tq, *w_arrival(e))
+        wb = slot[e] * SLOT
+        lo = run["pos"] - a
+        for i in range(G):
+            b = 4 * (k % 2) + i
+            if release[b]:
+                wait(tq, *release[b])
+            tq.matmul_mx(T.ps[:, b * BANK:b * BANK + n], T.wq[:, wb + i * TW:wb + (i + 1) * TW],
+                         T.ws[:, wb + i * TW:wb + (i + 1) * TW], rhs, rhs_s, True, True).then_inc(S["zb%d" % b], 1)
+            written[b] += 1
+            z = T.ps[:, b * BANK + lo:b * BANK + lo + run["cnt"]]
+            out = h[:, 4 * run["pos"] + i:4 * (run["pos"] + run["cnt"]):4]
+            if i % 2 == 0:
+                wait(sq, "zb%d" % b, written[b])
+                sq.activation(out, z, ActivationFunctionType.Relu, scale=CONST).then_inc(S[sem_a], 1)
+            else:
+                wait(vq, "zb%d" % b, written[b])
+                vq.tensor_scalar(out, z, 0.0, CONST, AluOpType.max, AluOpType.mult).then_inc(S[sem_a], 1)
+            release[b] = (sem_a, G)
+
+    def layer2(win, h, hq, hs, sem_q, out, sem_c):
+        runs = win["runs"]
+        for run in runs:
+            wait(vq, run["sem"], G)
+        vq.quantize_mx(hq[:, 0:win["W"]], hs[:, 0:win["W"]], h[:, 0:4 * win["W"]]).then_inc(S[sem_q], 1)
+        wait(tq, sem_q, 1)
+        first = 4 * ((jobs[0] - 1) % 2)
+        for j, run in enumerate(runs):
+            b = first + j
+            e, n, a = run["e"], run["n"], run["a"]
+            if e == r:
+                wait(tq, "q_w2", 1)
+            else:
+                wait(tq, *w_arrival(e))
+            if release[b]:
+                wait(tq, *release[b])
+            wb = slot[e] * SLOT + G * TW
+            tq.matmul_mx(T.ps[:, b * BANK:b * BANK + n], T.wq[:, wb:wb + TW], T.ws[:, wb:wb + TW],
+                         hq[:, a:a + n], hs[:, a:a + n], True, True).then_inc(S["zb%d" % b], 1)
+            written[b] += 1
+            lo = run["pos"] - a
+            p = T.ps[:, b * BANK + lo:b * BANK + lo + run["cnt"]]
+            o = out[:, run["pos"]:run["pos"] + run["cnt"]]
+            if j % 2 == 0:
+                wait(sq, "zb%d" % b, written[b])
+                sq.activation(o, p, ActivationFunctionType.Copy).then_inc(S[sem_c], 1)
+            else:
+                wait(vq, "zb%d" % b, written[b])
+                vq.tensor_copy(o, p).then_inc(S[sem_c], 1)
+            release[b] = (sem_c, len(runs))
+
+    for run in loc["runs"]:
+        if run["e"] == r:
+            layer1(run, False)
+    for run in sorted(cwin["runs"], key=lambda s: s["e"] != r):
+        layer1(run, True)
+    layer2(cwin, T.hx, T.hxq, T.hxs, "hq_x", T.px, "pc_x")
+    for run in loc["runs"]:
+        if run["e"] != r:
+            layer1(run, False)
+    layer2(loc, T.hl, T.hlq, T.hls, "hq_l", T.yl, "pc_l")
+
+    dst = T.cores[client]
+    assert topo.may_write(core, dst)
+    rid, pid, _ = topo.addr(dst)
+    m = topo.mask(core, dst)
+    g.wait_ge(S.pc_x, len(cwin["runs"]))
+    g.remote_dma(T.yr[:, 0:cwin["W"]], T.px[:, 0:cwin["W"]], S.ret, S.sent, pid, rid, m)
+    sent += _engines(m)
+    g.wait_ge(S.sent, sent)
+
+    wait(yq, "pc_l", len(loc["runs"]))
+    yq.dma_start(T.y[:, la:lb], T.yl[:, 0:loc["W"]]).then_inc(S.st, 16)
+    wait(yq, "ret", _engines(topo.mask(T.cores[server], core)))
+    yq.dma_start(T.y[:, xa:xb], T.yr[:, 0:crs["W"]]).then_inc(S.st, 16)
+    wait(yq, "st", 32)

@@ -8,6 +8,8 @@ SLOT = (G + 1) * TW
 PER_CHIP = 3
 CONST = 0.029
 BANK = 512
+HC = 1024
+RUNS = 2 * PER_CHIP
 
 SCRATCH = {
     "xt": ("sbuf", [128, 4 * NC], "bfloat16"),
@@ -19,20 +21,21 @@ SCRATCH = {
     "rs": ("sbuf", [128, NC], "uint8"),
     "wq": ("sbuf", [128, PER_CHIP * SLOT], "float8_e4m3fn_x4"),
     "ws": ("sbuf", [128, PER_CHIP * SLOT], "uint8"),
-    "hx": ("sbuf", [128, 4 * NC], "bfloat16"),
-    "hl": ("sbuf", [128, 4 * NC], "bfloat16"),
-    "hxq": ("sbuf", [128, NC], "float8_e4m3fn_x4"),
-    "hxs": ("sbuf", [128, NC], "uint8"),
-    "hlq": ("sbuf", [128, NC], "float8_e4m3fn_x4"),
-    "hls": ("sbuf", [128, NC], "uint8"),
+    "h": ("sbuf", [128, 4 * HC], "bfloat16"),
+    "hq": ("sbuf", [128, HC], "float8_e4m3fn_x4"),
+    "hs": ("sbuf", [128, HC], "uint8"),
     "px": ("sbuf", [128, NC], "float32"),
     "yl": ("sbuf", [128, NC], "float32"),
     "yr": ("sbuf", [128, NC], "float32"),
     "ps": ("psum", [128, 8 * BANK], "float32"),
 }
-SEMAPHORES = (["ld_xc", "ld_xl", "ld_w1", "ld_w2", "q_xc", "q_xl", "q_w1", "q_w2", "tok", "hq_x", "hq_l", "pc_x", "pc_l",
-               "ret", "sent", "st"]
-              + ["wa%d" % k for k in range(PER_CHIP)] + ["zb%d" % b for b in range(8)] + ["a%d" % s for s in range(2 * PER_CHIP)])
+SEMAPHORES = (["ld_xc", "ld_xl", "ld_w1", "ld_w2", "q_xc", "q_xl", "q_w1", "q_w2", "tok", "ms", "sent", "st", "st2"]
+              + ["%s%d" % (p, k) for p in ("wa", "ret") for k in range(PER_CHIP)] + ["zb%d" % b for b in range(8)]
+              + ["%s%d" % (p, k) for p in ("a", "hq", "pc") for k in range(RUNS)])
+
+
+def _back_order(win, worker):
+    return sorted(win["runs"], key=lambda s: (s["e"] != worker, -s["cnt"]))
 
 
 def _perms(a):
@@ -81,14 +84,17 @@ def _plan(T, topo):
             for w, c in zip(workers, p):
                 d = topo.die(T.cores[w])
                 port[d] = port.get(d, 0) + crs[c]["W"]
-            key = (max(port.values()), sorted((loc[w]["W"] + crs[c]["W"] for w, c in zip(workers, p)), reverse=True))
+            key = (max(port.values()),
+                   max(sum(s["cnt"] for s in crs[c]["runs"] if s["e"] != w) for w, c in zip(workers, p)),
+                   sorted((loc[w]["W"] + crs[c]["W"] for w, c in zip(workers, p)), reverse=True))
             if best is None or key < best[0]:
                 best = (key, p)
         for w, c in zip(workers, best[1]):
             worker[c] = w
     client = {w: c for c, w in worker.items()}
-    need = [set(s["e"] for s in loc[k]["runs"] + crs[client[k]]["runs"]) for k in range(n)]
-    return {"home": home, "loc": loc, "crs": crs, "worker": worker, "client": client, "need": need}
+    urgent = [set(s["e"] for s in crs[client[k]]["runs"]) for k in range(n)]
+    need = [urgent[k] | set(s["e"] for s in loc[k]["runs"]) for k in range(n)]
+    return {"home": home, "loc": loc, "crs": crs, "worker": worker, "client": client, "need": need, "urgent": urgent}
 
 
 def _engines(mask):
@@ -120,19 +126,35 @@ def rank_program(g, core, T, topo):
             seen[k] = val
             q.wait_ge(S[name], val)
 
+    order_l = sorted(loc["runs"], key=lambda s: s["e"] != r)
+    order_x = _back_order(cwin, r)
+    hb = 0
+    fills = 0
+    for k, run in enumerate(order_x + order_l):
+        run["id"] = k
+        run["hb"] = hb
+        hb += run["n"]
+        if run["cnt"] < run["n"]:
+            vq.memset(T.h[:, 4 * (run["hb"] + run["cnt"]):4 * hb], 0.0).then_inc(S.ms, 1)
+            fills += 1
+    assert hb <= HC
+
     yq.dma_start(T.xt[:, 4 * xa:4 * xb], T.x[:, 4 * xa:4 * xb]).then_inc(S.ld_xc, 16)
-    sq.dma_start(T.w1t[:], T.w1[:]).then_inc(S.ld_w1, 16)
-    sq.dma_start(T.w2t[:], T.w2[:]).then_inc(S.ld_w2, 16)
+    yq.dma_start(T.w1t[:], T.w1[:]).then_inc(S.ld_w1, 16)
+    yq.dma_start(T.w2t[:], T.w2[:]).then_inc(S.ld_w2, 16)
     yq.dma_start(T.xt[:, 4 * la:4 * lb], T.x[:, 4 * la:4 * lb]).then_inc(S.ld_xl, 16)
 
+    w2b = base + G * TW
     wait(vq, "ld_xc", 16)
     vq.quantize_mx(T.xq[:, xa:xb], T.xs[:, xa:xb], T.xt[:, 4 * xa:4 * xb]).then_inc(S.q_xc, 1)
     wait(vq, "ld_w1", 16)
-    vq.quantize_mx(T.wq[:, base:base + G * TW], T.ws[:, base:base + G * TW], T.w1t[:]).then_inc(S.q_w1, 1)
+    vq.quantize_mx(T.wq[:, base:w2b], T.ws[:, base:w2b], T.w1t[:]).then_inc(S.q_w1, 1)
     wait(vq, "ld_w2", 16)
-    vq.quantize_mx(T.wq[:, base + G * TW:base + SLOT], T.ws[:, base + G * TW:base + SLOT], T.w2t[:]).then_inc(S.q_w2, 1)
+    vq.quantize_mx(T.wq[:, w2b:base + SLOT], T.ws[:, w2b:base + SLOT], T.w2t[:]).then_inc(S.q_w2, 1)
     wait(vq, "ld_xl", 16)
     vq.quantize_mx(T.xq[:, la:lb], T.xs[:, la:lb], T.xt[:, 4 * la:4 * lb]).then_inc(S.q_xl, 1)
+    if fills:
+        wait(vq, "ms", fills)
 
     sent = 0
     dst = T.cores[server]
@@ -144,50 +166,54 @@ def rank_program(g, core, T, topo):
     g.remote_dma(T.rs[:, 0:crs["W"]], T.xs[:, xa:xb], S.tok, S.sent, pid, rid, m)
     sent += 2 * _engines(m)
 
-    takers = [k for k in mates if k != r and r in P["need"][k]]
-    if takers:
-        m = topo.mask(core, T.cores[takers[0]])
-        ids = []
-        for k in takers:
-            assert topo.may_write(core, T.cores[k])
-            m &= topo.mask(core, T.cores[k])
-            rid, pid, _ = topo.addr(T.cores[k])
-            ids.append(DstId(rid=rid, pnc=pid))
+    def w_way(e):
+        ways = []
+        for first in (True, False):
+            tk = [k for k in P["home"][e] if k != e and e in P["need"][k] and (e in P["urgent"][k]) == first]
+            if tk:
+                mm = topo.mask(T.cores[e], T.cores[tk[0]])
+                for k in tk:
+                    assert topo.may_write(T.cores[e], T.cores[k])
+                    mm &= topo.mask(T.cores[e], T.cores[k])
+                ways.append((tk, mm))
+        return ways
+
+    ways = w_way(r)
+    if ways:
         g.wait_ge(S.q_w1, 1)
         g.wait_ge(S.q_w2, 1)
+    for takers, m in ways:
+        ids = []
+        for k in takers:
+            rid, pid, _ = topo.addr(T.cores[k])
+            ids.append(DstId(rid=rid, pnc=pid))
         for ap in (T.wq[:, base:base + SLOT].bitcast(u8), T.ws[:, base:base + SLOT]):
             g.remote_dma_fused([RemoteDMATransfer(dst_ids=ids, dma_engine_mask=m, remote_sem=S["wa%d" % slot[r]],
                                                   srcs=[ap], dsts=[ap for _ in takers])], local_sem=S.sent)
             sent += _engines(m)
 
     def w_arrival(e):
-        src = T.cores[e]
-        mm = topo.mask(src, core)
-        for k in P["home"][e]:
-            if k != e and e in P["need"][k]:
-                mm &= topo.mask(src, T.cores[k])
-        return "wa%d" % slot[e], 2 * _engines(mm)
+        for tk, mm in w_way(e):
+            if r in tk:
+                return "wa%d" % slot[e], 2 * _engines(mm)
 
     tok_total = 2 * _engines(topo.mask(T.cores[client], core))
 
     written = [0] * 8
     release = [None] * 8
     jobs = [0]
-    nseg = [0]
 
     def layer1(run, away_side):
-        k = jobs[0]
+        run["set"] = 4 * (jobs[0] % 2)
         jobs[0] += 1
-        sem_a = "a%d" % nseg[0]
-        nseg[0] += 1
-        run["sem"] = sem_a
+        sem_a = "a%d" % run["id"]
         e, n, a = run["e"], run["n"], run["a"]
         if away_side:
             wait(tq, "tok", tok_total)
-            rhs, rhs_s, h = T.rq[:, a:a + n], T.rs[:, a:a + n], T.hx
+            rhs, rhs_s = T.rq[:, a:a + n], T.rs[:, a:a + n]
         else:
             wait(tq, "q_xl", 1)
-            rhs, rhs_s, h = T.xq[:, la + a:la + a + n], T.xs[:, la + a:la + a + n], T.hl
+            rhs, rhs_s = T.xq[:, la + a:la + a + n], T.xs[:, la + a:la + a + n]
         if e == r:
             wait(tq, "q_w1", 1)
         else:
@@ -195,14 +221,14 @@ def rank_program(g, core, T, topo):
         wb = slot[e] * SLOT
         lo = run["pos"] - a
         for i in range(G):
-            b = 4 * (k % 2) + i
+            b = run["set"] + i
             if release[b]:
                 wait(tq, *release[b])
             tq.matmul_mx(T.ps[:, b * BANK:b * BANK + n], T.wq[:, wb + i * TW:wb + (i + 1) * TW],
                          T.ws[:, wb + i * TW:wb + (i + 1) * TW], rhs, rhs_s, True, True).then_inc(S["zb%d" % b], 1)
             written[b] += 1
             z = T.ps[:, b * BANK + lo:b * BANK + lo + run["cnt"]]
-            out = h[:, 4 * run["pos"] + i:4 * (run["pos"] + run["cnt"]):4]
+            out = T.h[:, 4 * run["hb"] + i:4 * (run["hb"] + run["cnt"]):4]
             if i % 2 == 0:
                 wait(sq, "zb%d" % b, written[b])
                 sq.activation(out, z, ActivationFunctionType.Relu, scale=CONST).then_inc(S[sem_a], 1)
@@ -210,60 +236,71 @@ def rank_program(g, core, T, topo):
                 wait(vq, "zb%d" % b, written[b])
                 vq.tensor_scalar(out, z, 0.0, CONST, AluOpType.max, AluOpType.mult).then_inc(S[sem_a], 1)
             release[b] = (sem_a, G)
+        c0, c1 = run["hb"], run["hb"] + n
+        wait(vq, sem_a, G)
+        vq.quantize_mx(T.hq[:, c0:c1], T.hs[:, c0:c1], T.h[:, 4 * c0:4 * c1]).then_inc(S["hq%d" % run["id"]], 1)
 
-    def layer2(win, h, hq, hs, sem_q, out, sem_c):
-        runs = win["runs"]
-        for run in runs:
-            wait(vq, run["sem"], G)
-        vq.quantize_mx(hq[:, 0:win["W"]], hs[:, 0:win["W"]], h[:, 0:4 * win["W"]]).then_inc(S[sem_q], 1)
-        wait(tq, sem_q, 1)
-        first = 4 * ((jobs[0] - 1) % 2)
-        for j, run in enumerate(runs):
-            b = first + j
-            e, n, a = run["e"], run["n"], run["a"]
-            if e == r:
-                wait(tq, "q_w2", 1)
-            else:
-                wait(tq, *w_arrival(e))
-            if release[b]:
-                wait(tq, *release[b])
-            wb = slot[e] * SLOT + G * TW
-            tq.matmul_mx(T.ps[:, b * BANK:b * BANK + n], T.wq[:, wb:wb + TW], T.ws[:, wb:wb + TW],
-                         hq[:, a:a + n], hs[:, a:a + n], True, True).then_inc(S["zb%d" % b], 1)
-            written[b] += 1
-            lo = run["pos"] - a
-            p = T.ps[:, b * BANK + lo:b * BANK + lo + run["cnt"]]
-            o = out[:, run["pos"]:run["pos"] + run["cnt"]]
-            if j % 2 == 0:
-                wait(sq, "zb%d" % b, written[b])
-                sq.activation(o, p, ActivationFunctionType.Copy).then_inc(S[sem_c], 1)
-            else:
-                wait(vq, "zb%d" % b, written[b])
-                vq.tensor_copy(o, p).then_inc(S[sem_c], 1)
-            release[b] = (sem_c, len(runs))
+    def layer2(run, out, on_vector):
+        b = run["set"]
+        e, n = run["e"], run["n"]
+        c0, c1 = run["hb"], run["hb"] + n
+        wait(tq, "hq%d" % run["id"], 1)
+        if e == r:
+            wait(tq, "q_w2", 1)
+        wait(tq, *release[b])
+        wb = slot[e] * SLOT + G * TW
+        tq.matmul_mx(T.ps[:, b * BANK:b * BANK + n], T.wq[:, wb:wb + TW], T.ws[:, wb:wb + TW],
+                     T.hq[:, c0:c1], T.hs[:, c0:c1], True, True).then_inc(S["zb%d" % b], 1)
+        written[b] += 1
+        o, p = out[:, run["pos"]:run["pos"] + run["cnt"]], T.ps[:, b * BANK:b * BANK + run["cnt"]]
+        if on_vector:
+            wait(vq, "zb%d" % b, written[b])
+            vq.tensor_copy(o, p).then_inc(S["pc%d" % run["id"]], 1)
+        else:
+            wait(sq, "zb%d" % b, written[b])
+            sq.activation(o, p, ActivationFunctionType.Copy).then_inc(S["pc%d" % run["id"]], 1)
+        release[b] = ("pc%d" % run["id"], 1)
 
-    for run in loc["runs"]:
-        if run["e"] == r:
-            layer1(run, False)
-    for run in sorted(cwin["runs"], key=lambda s: s["e"] != r):
-        layer1(run, True)
-    layer2(cwin, T.hx, T.hxq, T.hxs, "hq_x", T.px, "pc_x")
-    for run in loc["runs"]:
-        if run["e"] != r:
-            layer1(run, False)
-    layer2(loc, T.hl, T.hlq, T.hls, "hq_l", T.yl, "pc_l")
+    def batch(runs, away_side, out):
+        for k in range(0, len(runs), 2):
+            for run in runs[k:k + 2]:
+                layer1(run, away_side)
+            for j, run in enumerate(runs[k:k + 2]):
+                layer2(run, out, j == 1)
+
+    batch([s for s in order_l if s["e"] == r], False, T.yl)
+    batch(order_x, True, T.px)
+    batch([s for s in order_l if s["e"] != r], False, T.yl)
 
     dst = T.cores[client]
     assert topo.may_write(core, dst)
     rid, pid, _ = topo.addr(dst)
     m = topo.mask(core, dst)
-    g.wait_ge(S.pc_x, len(cwin["runs"]))
-    g.remote_dma(T.yr[:, 0:cwin["W"]], T.px[:, 0:cwin["W"]], S.ret, S.sent, pid, rid, m)
-    sent += _engines(m)
+    for k, run in enumerate(order_x):
+        c0, c1 = run["pos"], run["pos"] + run["cnt"]
+        g.wait_ge(S["pc%d" % run["id"]], 1)
+        g.remote_dma(T.yr[:, c0:c1], T.px[:, c0:c1], S["ret%d" % k], S.sent, pid, rid, m)
+        sent += _engines(m)
     g.wait_ge(S.sent, sent)
 
-    wait(yq, "pc_l", len(loc["runs"]))
-    yq.dma_start(T.y[:, la:lb], T.yl[:, 0:loc["W"]]).then_inc(S.st, 16)
-    wait(yq, "ret", _engines(topo.mask(T.cores[server], core)))
-    yq.dma_start(T.y[:, xa:xb], T.yr[:, 0:crs["W"]]).then_inc(S.st, 16)
-    wait(yq, "st", 32)
+    n_sync = 0
+    n_scal = 0
+    for run in order_l:
+        c0, c1 = run["pos"], run["pos"] + run["cnt"]
+        if run["e"] == r:
+            wait(yq, "pc%d" % run["id"], 1)
+            yq.dma_start(T.y[:, la + c0:la + c1], T.yl[:, c0:c1]).then_inc(S.st, 16)
+            n_sync += 16
+        else:
+            wait(sq, "pc%d" % run["id"], 1)
+            sq.dma_start(T.y[:, la + c0:la + c1], T.yl[:, c0:c1]).then_inc(S.st2, 16)
+            n_scal += 16
+    back = _engines(topo.mask(T.cores[server], core))
+    for k, run in enumerate(_back_order(crs, server)):
+        c0, c1 = run["pos"], run["pos"] + run["cnt"]
+        wait(yq, "ret%d" % k, back)
+        yq.dma_start(T.y[:, xa + c0:xa + c1], T.yr[:, c0:c1]).then_inc(S.st, 16)
+        n_sync += 16
+    wait(yq, "st", n_sync)
+    if n_scal:
+        wait(sq, "st2", n_scal)

@@ -5,11 +5,13 @@ NC = 512
 TW = 128
 G = 4
 SLOT = (G + 1) * TW
-PER_CHIP = 3
+NSLOT = 3
 CONST = 0.029
 BANK = 512
 HC = 1024
-RUNS = 2 * PER_CHIP
+RUNS = 6
+NEXP = 6
+GO = ((0, 2), (1, 2), (2, 1), (2, 3), (3, 4), (3, 5), (4, 0), (5, 4))
 
 SCRATCH = {
     "xt": ("sbuf", [128, 4 * NC], "bfloat16"),
@@ -19,8 +21,8 @@ SCRATCH = {
     "xs": ("sbuf", [128, NC], "uint8"),
     "rq": ("sbuf", [128, NC], "float8_e4m3fn_x4"),
     "rs": ("sbuf", [128, NC], "uint8"),
-    "wq": ("sbuf", [128, PER_CHIP * SLOT], "float8_e4m3fn_x4"),
-    "ws": ("sbuf", [128, PER_CHIP * SLOT], "uint8"),
+    "wq": ("sbuf", [128, NSLOT * SLOT], "float8_e4m3fn_x4"),
+    "ws": ("sbuf", [128, NSLOT * SLOT], "uint8"),
     "h": ("sbuf", [128, 4 * HC], "bfloat16"),
     "hq": ("sbuf", [128, HC], "float8_e4m3fn_x4"),
     "hs": ("sbuf", [128, HC], "uint8"),
@@ -29,94 +31,101 @@ SCRATCH = {
     "yr": ("sbuf", [128, NC], "float32"),
     "ps": ("psum", [128, 8 * BANK], "float32"),
 }
-SEMAPHORES = (["ld_xc", "ld_xl", "ld_w1", "ld_w2", "q_xc", "q_xl", "q_w1", "q_w2", "tok", "ms", "sent", "st", "st2"]
-              + ["%s%d" % (p, k) for p in ("wa", "ret") for k in range(PER_CHIP)] + ["zb%d" % b for b in range(8)]
+SEMAPHORES = (["ld_w1", "ld_w2", "q_w1", "q_w2", "ms", "sent", "st", "st2", "tok0", "tok1"]
+              + ["%s%d" % (p, k) for p in ("ld_x", "q_x") for k in range(4)]
+              + ["%s%d" % (p, k) for p in ("wa", "ret") for k in range(NEXP)] + ["zb%d" % b for b in range(8)]
               + ["%s%d" % (p, k) for p in ("a", "hq", "pc") for k in range(RUNS)])
 
 
-def _back_order(win, worker):
-    return sorted(win["runs"], key=lambda s: (s["e"] != worker, -s["cnt"]))
+def _blocks(a, b):
+    return set(range(a // TW, (b - 1) // TW + 1))
 
 
-def _perms(a):
-    if len(a) <= 1:
-        return [list(a)]
-    out = []
-    for i in range(len(a)):
-        for p in _perms(a[:i] + a[i + 1:]):
-            out.append([a[i]] + p)
-    return out
-
-
-def _window(cnt_row, off_row, experts):
-    assert experts == list(range(experts[0], experts[-1] + 1))
-    base = off_row[experts[0]]
-    width = off_row[experts[-1] + 1] - base
-    assert TW <= width <= NC
-    runs = []
-    for e in experts:
-        c = cnt_row[e]
-        if c:
-            pos = off_row[e] - base
-            n = max(c, TW)
-            runs.append({"e": e, "cnt": c, "pos": pos, "a": min(pos, width - n), "n": n})
-    return {"base": base, "W": width, "runs": runs}
-
-
-def _plan(T, topo):
+def _plan(T):
     cnt = T.tables["CNT"]
     n = len(T.cores)
     off = [[sum(row[:e]) for e in range(n + 1)] for row in cnt]
-    chip = [topo.chip(c) for c in T.cores]
-    home = [[k for k in range(n) if chip[k] == chip[j]] for j in range(n)]
-    away = [[k for k in range(n) if chip[k] != chip[j]] for j in range(n)]
-    loc = [_window(cnt[j], off[j], home[j]) for j in range(n)]
-    crs = [_window(cnt[j], off[j], away[j]) for j in range(n)]
-    worker = {}
-    for ch in sorted(set(chip)):
-        workers = [k for k in range(n) if chip[k] == ch]
-        clients = [k for k in range(n) if chip[k] != ch]
-        best = None
-        for p in _perms(clients):
-            if any(sum(s["n"] for s in loc[w]["runs"] + crs[c]["runs"]) < NC for w, c in zip(workers, p)):
-                continue
-            port = {}
-            for w, c in zip(workers, p):
-                d = topo.die(T.cores[w])
-                port[d] = port.get(d, 0) + crs[c]["W"]
-            key = (max(port.values()),
-                   max(sum(s["cnt"] for s in crs[c]["runs"] if s["e"] != w) for w, c in zip(workers, p)),
-                   sorted((loc[w]["W"] + crs[c]["W"] for w, c in zip(workers, p)), reverse=True))
-            if best is None or key < best[0]:
-                best = (key, p)
-        for w, c in zip(workers, best[1]):
-            worker[c] = w
-    client = {w: c for c, w in worker.items()}
-    urgent = [set(s["e"] for s in crs[client[k]]["runs"]) for k in range(n)]
-    need = [urgent[k] | set(s["e"] for s in loc[k]["runs"]) for k in range(n)]
-    return {"home": home, "loc": loc, "crs": crs, "worker": worker, "client": client, "need": need, "urgent": urgent}
+    go = set(GO)
+    for j, e in go:
+        assert j != e and cnt[j][e]
+    src = [[j for j in range(n) if j != e and cnt[j][e] and (j, e) not in go] for e in range(n)]
+    total = [sum(cnt[j][e] for j in src[e]) for e in range(n)]
+    urgent = [set() for _ in range(n)]
+    for e in range(n):
+        for j in src[e]:
+            urgent[j] |= _blocks(off[j][e], off[j][e + 1])
+    send = {}
+    groups = []
+    for e in range(n):
+        order = sorted(src[e], key=lambda j: -cnt[j][e])
+        pad = max(0, TW - total[e]) if order else 0
+        if pad:
+            fit = [j for j in order if off[j][e + 1] + pad <= NC]
+            k = min(fit, key=lambda j: len(_blocks(off[j][e], off[j][e + 1] + pad) - urgent[j]))
+            order.remove(k)
+            order.append(k)
+            urgent[k] |= _blocks(off[k][e], off[k][e + 1] + pad)
+        pos = 0
+        for j in order:
+            w = cnt[j][e] + (pad if j == order[-1] else 0)
+            send[(j, e)] = {"a": off[j][e], "w": w, "cnt": cnt[j][e], "pos": pos, "grp": 0}
+            pos += w
+        cut = None
+        for k in range(1, len(order)):
+            left = sum(cnt[j][e] for j in order[:k])
+            if left >= TW and total[e] - left >= TW:
+                cut = k
+        if cut is None:
+            groups.append([order] if order else [])
+        else:
+            groups.append([order[:cut], order[cut:]])
+            for j in order[cut:]:
+                send[(j, e)]["grp"] = 1
+    pieces = []
+    for j in range(n):
+        mine = sorted([e for e in range(n) if (j, e) in send], key=lambda e: -total[e])
+        first, rest = [], []
+        for want, out in ((True, first), (False, rest)):
+            k = 0
+            while k < NC // TW:
+                if (k in urgent[j]) == want:
+                    k0 = k
+                    while k < NC // TW and (k in urgent[j]) == want:
+                        k += 1
+                    out.append((k0 * TW, k * TW))
+                else:
+                    k += 1
+
+        def rank_of_piece(p):
+            return min(i for i, e in enumerate(mine)
+                       if send[(j, e)]["a"] < p[1] and p[0] < send[(j, e)]["a"] + send[(j, e)]["w"])
+        first.sort(key=rank_of_piece)
+        pieces.append({"first": first, "rest": rest, "mine": mine})
+    return {"cnt": cnt, "off": off, "send": send, "groups": groups, "pieces": pieces, "total": total}
 
 
 def _engines(mask):
     return bin(mask).count("1")
 
 
+def _slot(j, e):
+    if e == j:
+        return 0
+    return 1 + sorted(e2 for (j2, e2) in GO if j2 == j).index(e)
+
+
 def rank_program(g, core, T, topo):
     r = T.rank_of(core)
     if r is None:
         return
-    P = _plan(T, topo)
+    P = _plan(T)
     S = T.sem
     tq, vq, sq, yq = g.tensor, g.vector, g.scalar, g.sync
     u8 = dt.uint8
-    mates = P["home"][r]
-    slot = {e: k for k, e in enumerate(mates)}
-    loc, crs = P["loc"][r], P["crs"][r]
-    client, server = P["client"][r], P["worker"][r]
-    cwin = P["crs"][client]
-    xa, xb = crs["base"], crs["base"] + crs["W"]
-    la, lb = loc["base"], loc["base"] + loc["W"]
-    base = slot[r] * SLOT
+    cnt, off, send = P["cnt"], P["off"], P["send"]
+    n_ranks = len(T.cores)
+    pcs = P["pieces"][r]["first"] + P["pieces"][r]["rest"]
+    n_first = len(P["pieces"][r]["first"])
 
     seen = {}
 
@@ -126,11 +135,44 @@ def rank_program(g, core, T, topo):
             seen[k] = val
             q.wait_ge(S[name], val)
 
-    order_l = sorted(loc["runs"], key=lambda s: s["e"] != r)
-    order_x = _back_order(cwin, r)
+    def wait_x(q, a, b):
+        for k, p in enumerate(pcs):
+            if p[0] < b and a < p[1]:
+                wait(q, "q_x%d" % k, 1)
+
+    def w_way(e):
+        ways = []
+        takers = [j for (j, e2) in GO if e2 == e]
+        for ch in sorted(set(topo.chip(T.cores[j]) for j in takers)):
+            tk = sorted(j for j in takers if topo.chip(T.cores[j]) == ch)
+            mm = topo.mask(T.cores[e], T.cores[tk[0]])
+            for k in tk:
+                assert topo.may_write(T.cores[e], T.cores[k])
+                mm &= topo.mask(T.cores[e], T.cores[k])
+            ways.append((tk, mm))
+        return ways
+
+    def own_run(e):
+        c = cnt[r][e]
+        n = max(c, TW)
+        a = min(off[r][e], NC - n)
+        return {"e": e, "cnt": c, "n": n, "a": a, "lo": off[r][e] - a, "oc": off[r][e], "afar": False}
+
+    diag = [own_run(r)] if cnt[r][r] else []
+    here = topo.chip(core)
+    wruns = [own_run(e) for e in sorted((e for (j, e) in GO if j == r),
+                                        key=lambda e: (topo.chip(T.cores[e]) != here, -cnt[r][e]))]
+    truns = []
+    for gi, grp in enumerate(P["groups"][r]):
+        p0 = send[(grp[0], r)]["pos"]
+        truns.append({"e": r, "cnt": sum(cnt[j][r] for j in grp), "n": sum(send[(j, r)]["w"] for j in grp), "a": p0,
+                      "lo": 0, "oc": p0, "afar": True, "grp": gi, "from": grp,
+                      "tokn": sum(2 * _engines(topo.mask(T.cores[j], core)) for j in grp)})
+    assert sum(s["n"] for s in diag + truns + wruns) >= NC
+
     hb = 0
     fills = 0
-    for k, run in enumerate(order_x + order_l):
+    for k, run in enumerate(diag + truns + wruns):
         run["id"] = k
         run["hb"] = hb
         hb += run["n"]
@@ -139,87 +181,92 @@ def rank_program(g, core, T, topo):
             fills += 1
     assert hb <= HC
 
-    yq.dma_start(T.xt[:, 4 * xa:4 * xb], T.x[:, 4 * xa:4 * xb]).then_inc(S.ld_xc, 16)
+    def load_x(k):
+        a, b = pcs[k]
+        yq.dma_start(T.xt[:, 4 * a:4 * b], T.x[:, 4 * a:4 * b]).then_inc(S["ld_x%d" % k], 16)
+
+    def pack_x(k):
+        a, b = pcs[k]
+        wait(vq, "ld_x%d" % k, 16)
+        vq.quantize_mx(T.xq[:, a:b], T.xs[:, a:b], T.xt[:, 4 * a:4 * b]).then_inc(S["q_x%d" % k], 1)
+
+    for k in range(n_first):
+        load_x(k)
     yq.dma_start(T.w1t[:], T.w1[:]).then_inc(S.ld_w1, 16)
     yq.dma_start(T.w2t[:], T.w2[:]).then_inc(S.ld_w2, 16)
-    yq.dma_start(T.xt[:, 4 * la:4 * lb], T.x[:, 4 * la:4 * lb]).then_inc(S.ld_xl, 16)
+    for k in range(n_first, len(pcs)):
+        load_x(k)
 
-    w2b = base + G * TW
-    wait(vq, "ld_xc", 16)
-    vq.quantize_mx(T.xq[:, xa:xb], T.xs[:, xa:xb], T.xt[:, 4 * xa:4 * xb]).then_inc(S.q_xc, 1)
+    w2b = G * TW
+    for k in range(n_first):
+        pack_x(k)
     wait(vq, "ld_w1", 16)
-    vq.quantize_mx(T.wq[:, base:w2b], T.ws[:, base:w2b], T.w1t[:]).then_inc(S.q_w1, 1)
+    vq.quantize_mx(T.wq[:, 0:w2b], T.ws[:, 0:w2b], T.w1t[:]).then_inc(S.q_w1, 1)
     wait(vq, "ld_w2", 16)
-    vq.quantize_mx(T.wq[:, w2b:base + SLOT], T.ws[:, w2b:base + SLOT], T.w2t[:]).then_inc(S.q_w2, 1)
-    wait(vq, "ld_xl", 16)
-    vq.quantize_mx(T.xq[:, la:lb], T.xs[:, la:lb], T.xt[:, 4 * la:4 * lb]).then_inc(S.q_xl, 1)
+    vq.quantize_mx(T.wq[:, w2b:SLOT], T.ws[:, w2b:SLOT], T.w2t[:]).then_inc(S.q_w2, 1)
+    for k in range(n_first, len(pcs)):
+        pack_x(k)
     if fills:
         wait(vq, "ms", fills)
 
     sent = 0
-    dst = T.cores[server]
-    assert topo.may_write(core, dst)
-    rid, pid, _ = topo.addr(dst)
-    m = topo.mask(core, dst)
-    g.wait_ge(S.q_xc, 1)
-    g.remote_dma(T.rq[:, 0:crs["W"]].bitcast(u8), T.xq[:, xa:xb].bitcast(u8), S.tok, S.sent, pid, rid, m)
-    g.remote_dma(T.rs[:, 0:crs["W"]], T.xs[:, xa:xb], S.tok, S.sent, pid, rid, m)
-    sent += 2 * _engines(m)
-
-    def w_way(e):
-        ways = []
-        for first in (True, False):
-            tk = [k for k in P["home"][e] if k != e and e in P["need"][k] and (e in P["urgent"][k]) == first]
-            if tk:
-                mm = topo.mask(T.cores[e], T.cores[tk[0]])
-                for k in tk:
-                    assert topo.may_write(T.cores[e], T.cores[k])
-                    mm &= topo.mask(T.cores[e], T.cores[k])
-                ways.append((tk, mm))
-        return ways
+    for e in P["pieces"][r]["mine"]:
+        s = send[(r, e)]
+        dst = T.cores[e]
+        assert topo.may_write(core, dst)
+        rid, pid, _ = topo.addr(dst)
+        m = topo.mask(core, dst)
+        a, w, p = s["a"], s["w"], s["pos"]
+        wait_x(g, a, a + w)
+        tok = S["tok%d" % s["grp"]]
+        g.remote_dma(T.rq[:, p:p + w].bitcast(u8), T.xq[:, a:a + w].bitcast(u8), tok, S.sent, pid, rid, m)
+        g.remote_dma(T.rs[:, p:p + w], T.xs[:, a:a + w], tok, S.sent, pid, rid, m)
+        sent += 2 * _engines(m)
 
     ways = w_way(r)
     if ways:
-        g.wait_ge(S.q_w1, 1)
-        g.wait_ge(S.q_w2, 1)
+        wait(g, "q_w1", 1)
+        wait(g, "q_w2", 1)
     for takers, m in ways:
         ids = []
         for k in takers:
             rid, pid, _ = topo.addr(T.cores[k])
             ids.append(DstId(rid=rid, pnc=pid))
-        for ap in (T.wq[:, base:base + SLOT].bitcast(u8), T.ws[:, base:base + SLOT]):
-            g.remote_dma_fused([RemoteDMATransfer(dst_ids=ids, dma_engine_mask=m, remote_sem=S["wa%d" % slot[r]],
-                                                  srcs=[ap], dsts=[ap for _ in takers])], local_sem=S.sent)
-            sent += _engines(m)
+        bases = [_slot(k, r) * SLOT for k in takers]
+        g.remote_dma_fused([RemoteDMATransfer(dst_ids=ids, dma_engine_mask=m, remote_sem=S["wa%d" % r],
+                                              srcs=[T.wq[:, 0:SLOT].bitcast(u8)],
+                                              dsts=[T.wq[:, b:b + SLOT].bitcast(u8) for b in bases])], local_sem=S.sent)
+        g.remote_dma_fused([RemoteDMATransfer(dst_ids=ids, dma_engine_mask=m, remote_sem=S["wa%d" % r],
+                                              srcs=[T.ws[:, 0:SLOT]],
+                                              dsts=[T.ws[:, b:b + SLOT] for b in bases])], local_sem=S.sent)
+        sent += 2 * _engines(m)
 
     def w_arrival(e):
         for tk, mm in w_way(e):
             if r in tk:
-                return "wa%d" % slot[e], 2 * _engines(mm)
-
-    tok_total = 2 * _engines(topo.mask(T.cores[client], core))
+                return "wa%d" % e, 2 * _engines(mm)
 
     written = [0] * 8
     release = [None] * 8
     jobs = [0]
 
-    def layer1(run, away_side):
+    def layer1(run):
         run["set"] = 4 * (jobs[0] % 2)
         jobs[0] += 1
         sem_a = "a%d" % run["id"]
         e, n, a = run["e"], run["n"], run["a"]
-        if away_side:
-            wait(tq, "tok", tok_total)
+        if run["afar"]:
+            wait(tq, "tok%d" % run["grp"], run["tokn"])
             rhs, rhs_s = T.rq[:, a:a + n], T.rs[:, a:a + n]
         else:
-            wait(tq, "q_xl", 1)
-            rhs, rhs_s = T.xq[:, la + a:la + a + n], T.xs[:, la + a:la + a + n]
+            wait_x(tq, a, a + n)
+            rhs, rhs_s = T.xq[:, a:a + n], T.xs[:, a:a + n]
         if e == r:
             wait(tq, "q_w1", 1)
         else:
             wait(tq, *w_arrival(e))
-        wb = slot[e] * SLOT
-        lo = run["pos"] - a
+        wb = _slot(r, e) * SLOT
+        lo = run["lo"]
         for i in range(G):
             b = run["set"] + i
             if release[b]:
@@ -248,11 +295,11 @@ def rank_program(g, core, T, topo):
         if e == r:
             wait(tq, "q_w2", 1)
         wait(tq, *release[b])
-        wb = slot[e] * SLOT + G * TW
+        wb = _slot(r, e) * SLOT + G * TW
         tq.matmul_mx(T.ps[:, b * BANK:b * BANK + n], T.wq[:, wb:wb + TW], T.ws[:, wb:wb + TW],
                      T.hq[:, c0:c1], T.hs[:, c0:c1], True, True).then_inc(S["zb%d" % b], 1)
         written[b] += 1
-        o, p = out[:, run["pos"]:run["pos"] + run["cnt"]], T.ps[:, b * BANK:b * BANK + run["cnt"]]
+        o, p = out[:, run["oc"]:run["oc"] + run["cnt"]], T.ps[:, b * BANK:b * BANK + run["cnt"]]
         if on_vector:
             wait(vq, "zb%d" % b, written[b])
             vq.tensor_copy(o, p).then_inc(S["pc%d" % run["id"]], 1)
@@ -261,46 +308,49 @@ def rank_program(g, core, T, topo):
             sq.activation(o, p, ActivationFunctionType.Copy).then_inc(S["pc%d" % run["id"]], 1)
         release[b] = ("pc%d" % run["id"], 1)
 
-    def batch(runs, away_side, out):
+    def batch(runs, out):
         for k in range(0, len(runs), 2):
             for run in runs[k:k + 2]:
-                layer1(run, away_side)
+                layer1(run)
             for j, run in enumerate(runs[k:k + 2]):
                 layer2(run, out, j == 1)
 
-    batch([s for s in order_l if s["e"] == r], False, T.yl)
-    batch(order_x, True, T.px)
-    batch([s for s in order_l if s["e"] != r], False, T.yl)
+    batch(diag, T.yl)
+    batch(truns, T.px)
+    batch(wruns, T.yl)
 
-    dst = T.cores[client]
-    assert topo.may_write(core, dst)
-    rid, pid, _ = topo.addr(dst)
-    m = topo.mask(core, dst)
-    for k, run in enumerate(order_x):
-        c0, c1 = run["pos"], run["pos"] + run["cnt"]
-        g.wait_ge(S["pc%d" % run["id"]], 1)
-        g.remote_dma(T.yr[:, c0:c1], T.px[:, c0:c1], S["ret%d" % k], S.sent, pid, rid, m)
-        sent += _engines(m)
+    for run in truns:
+        wait(g, "pc%d" % run["id"], 1)
+        for j in run["from"]:
+            s = send[(j, r)]
+            dst = T.cores[j]
+            assert topo.may_write(core, dst)
+            rid, pid, _ = topo.addr(dst)
+            m = topo.mask(core, dst)
+            g.remote_dma(T.yr[:, s["a"]:s["a"] + s["cnt"]], T.px[:, s["pos"]:s["pos"] + s["cnt"]],
+                         S["ret%d" % r], S.sent, pid, rid, m)
+            sent += _engines(m)
     g.wait_ge(S.sent, sent)
 
     n_sync = 0
     n_scal = 0
-    for run in order_l:
-        c0, c1 = run["pos"], run["pos"] + run["cnt"]
-        if run["e"] == r:
-            wait(yq, "pc%d" % run["id"], 1)
-            yq.dma_start(T.y[:, la + c0:la + c1], T.yl[:, c0:c1]).then_inc(S.st, 16)
-            n_sync += 16
-        else:
-            wait(sq, "pc%d" % run["id"], 1)
-            sq.dma_start(T.y[:, la + c0:la + c1], T.yl[:, c0:c1]).then_inc(S.st2, 16)
-            n_scal += 16
-    back = _engines(topo.mask(T.cores[server], core))
-    for k, run in enumerate(_back_order(crs, server)):
-        c0, c1 = run["pos"], run["pos"] + run["cnt"]
-        wait(yq, "ret%d" % k, back)
-        yq.dma_start(T.y[:, xa + c0:xa + c1], T.yr[:, c0:c1]).then_inc(S.st, 16)
+    for run in diag:
+        c0, c1 = run["oc"], run["oc"] + run["cnt"]
+        wait(yq, "pc%d" % run["id"], 1)
+        yq.dma_start(T.y[:, c0:c1], T.yl[:, c0:c1]).then_inc(S.st, 16)
+        n_sync += 16
+    for run in wruns:
+        c0, c1 = run["oc"], run["oc"] + run["cnt"]
+        wait(sq, "pc%d" % run["id"], 1)
+        sq.dma_start(T.y[:, c0:c1], T.yl[:, c0:c1]).then_inc(S.st2, 16)
+        n_scal += 16
+    for e in reversed(P["pieces"][r]["mine"]):
+        s = send[(r, e)]
+        c0, c1 = s["a"], s["a"] + s["cnt"]
+        wait(yq, "ret%d" % e, _engines(topo.mask(T.cores[e], core)))
+        yq.dma_start(T.y[:, c0:c1], T.yr[:, c0:c1]).then_inc(S.st, 16)
         n_sync += 16
     wait(yq, "st", n_sync)
     if n_scal:
         wait(sq, "st2", n_scal)
+    assert n_ranks == NEXP

@@ -33,7 +33,7 @@ SCRATCH = {
 }
 SEMAPHORES = (["ld_w1", "ld_w2", "q_w1", "q_w2", "ms", "sent", "st", "st2", "tok0", "tok1"]
               + ["%s%d" % (p, k) for p in ("ld_x", "q_x") for k in range(4)]
-              + ["%s%d" % (p, k) for p in ("wa", "ret") for k in range(NEXP)] + ["zb%d" % b for b in range(8)]
+              + ["%s%d" % (p, k) for p in ("wa", "wb", "ret") for k in range(NEXP)] + ["zb%d" % b for b in range(8)]
               + ["%s%d" % (p, k) for p in ("a", "hq", "pc") for k in range(RUNS)])
 
 
@@ -140,6 +140,13 @@ def rank_program(g, core, T, topo):
             if p[0] < b and a < p[1]:
                 wait(q, "q_x%d" % k, 1)
 
+    def short_mask(c):
+        mm = None
+        for d in T.cores:
+            if d != c:
+                mm = topo.mask(c, d) if mm is None else mm & topo.mask(c, d)
+        return mm
+
     def w_way(e):
         ways = []
         takers = [j for (j, e2) in GO if e2 == e]
@@ -167,7 +174,7 @@ def rank_program(g, core, T, topo):
         p0 = send[(grp[0], r)]["pos"]
         truns.append({"e": r, "cnt": sum(cnt[j][r] for j in grp), "n": sum(send[(j, r)]["w"] for j in grp), "a": p0,
                       "lo": 0, "oc": p0, "afar": True, "grp": gi, "from": grp,
-                      "tokn": sum(2 * _engines(topo.mask(T.cores[j], core)) for j in grp)})
+                      "tokn": sum(2 * _engines(short_mask(T.cores[j])) for j in grp)})
     assert sum(s["n"] for s in diag + truns + wruns) >= NC
 
     hb = 0
@@ -210,41 +217,42 @@ def rank_program(g, core, T, topo):
         wait(vq, "ms", fills)
 
     sent = 0
+    m_short = short_mask(core)
     for e in P["pieces"][r]["mine"]:
         s = send[(r, e)]
         dst = T.cores[e]
         assert topo.may_write(core, dst)
         rid, pid, _ = topo.addr(dst)
-        m = topo.mask(core, dst)
         a, w, p = s["a"], s["w"], s["pos"]
         wait_x(g, a, a + w)
         tok = S["tok%d" % s["grp"]]
-        g.remote_dma(T.rq[:, p:p + w].bitcast(u8), T.xq[:, a:a + w].bitcast(u8), tok, S.sent, pid, rid, m)
-        g.remote_dma(T.rs[:, p:p + w], T.xs[:, a:a + w], tok, S.sent, pid, rid, m)
-        sent += 2 * _engines(m)
+        g.remote_dma(T.rq[:, p:p + w].bitcast(u8), T.xq[:, a:a + w].bitcast(u8), tok, S.sent, pid, rid, m_short)
+        g.remote_dma(T.rs[:, p:p + w], T.xs[:, a:a + w], tok, S.sent, pid, rid, m_short)
+        sent += 2 * _engines(m_short)
 
     ways = w_way(r)
-    if ways:
-        wait(g, "q_w1", 1)
-        wait(g, "q_w2", 1)
-    for takers, m in ways:
-        ids = []
-        for k in takers:
-            rid, pid, _ = topo.addr(T.cores[k])
-            ids.append(DstId(rid=rid, pnc=pid))
-        bases = [_slot(k, r) * SLOT for k in takers]
-        g.remote_dma_fused([RemoteDMATransfer(dst_ids=ids, dma_engine_mask=m, remote_sem=S["wa%d" % r],
-                                              srcs=[T.wq[:, 0:SLOT].bitcast(u8)],
-                                              dsts=[T.wq[:, b:b + SLOT].bitcast(u8) for b in bases])], local_sem=S.sent)
-        g.remote_dma_fused([RemoteDMATransfer(dst_ids=ids, dma_engine_mask=m, remote_sem=S["wa%d" % r],
-                                              srcs=[T.ws[:, 0:SLOT]],
-                                              dsts=[T.ws[:, b:b + SLOT] for b in bases])], local_sem=S.sent)
-        sent += 2 * _engines(m)
+    for c0, c1, name, ready in ((0, w2b, "wa", "q_w1"), (w2b, SLOT, "wb", "q_w2")):
+        if ways:
+            wait(g, ready, 1)
+        for takers, m in ways:
+            ids = []
+            for k in takers:
+                rid, pid, _ = topo.addr(T.cores[k])
+                ids.append(DstId(rid=rid, pnc=pid))
+            bases = [_slot(k, r) * SLOT for k in takers]
+            g.remote_dma_fused([RemoteDMATransfer(dst_ids=ids, dma_engine_mask=m, remote_sem=S["%s%d" % (name, r)],
+                                                  srcs=[T.wq[:, c0:c1].bitcast(u8)],
+                                                  dsts=[T.wq[:, b + c0:b + c1].bitcast(u8) for b in bases])],
+                               local_sem=S.sent)
+            g.remote_dma_fused([RemoteDMATransfer(dst_ids=ids, dma_engine_mask=m, remote_sem=S["%s%d" % (name, r)],
+                                                  srcs=[T.ws[:, c0:c1]],
+                                                  dsts=[T.ws[:, b + c0:b + c1] for b in bases])], local_sem=S.sent)
+            sent += 2 * _engines(m)
 
-    def w_arrival(e):
+    def w_arrival(e, name):
         for tk, mm in w_way(e):
             if r in tk:
-                return "wa%d" % e, 2 * _engines(mm)
+                return "%s%d" % (name, e), 2 * _engines(mm)
 
     written = [0] * 8
     release = [None] * 8
@@ -264,7 +272,7 @@ def rank_program(g, core, T, topo):
         if e == r:
             wait(tq, "q_w1", 1)
         else:
-            wait(tq, *w_arrival(e))
+            wait(tq, *w_arrival(e, "wa"))
         wb = _slot(r, e) * SLOT
         lo = run["lo"]
         for i in range(G):
@@ -294,6 +302,8 @@ def rank_program(g, core, T, topo):
         wait(tq, "hq%d" % run["id"], 1)
         if e == r:
             wait(tq, "q_w2", 1)
+        else:
+            wait(tq, *w_arrival(e, "wb"))
         wait(tq, *release[b])
         wb = _slot(r, e) * SLOT + G * TW
         tq.matmul_mx(T.ps[:, b * BANK:b * BANK + n], T.wq[:, wb:wb + TW], T.ws[:, wb:wb + TW],
@@ -326,10 +336,9 @@ def rank_program(g, core, T, topo):
             dst = T.cores[j]
             assert topo.may_write(core, dst)
             rid, pid, _ = topo.addr(dst)
-            m = topo.mask(core, dst)
             g.remote_dma(T.yr[:, s["a"]:s["a"] + s["cnt"]], T.px[:, s["pos"]:s["pos"] + s["cnt"]],
-                         S["ret%d" % r], S.sent, pid, rid, m)
-            sent += _engines(m)
+                         S["ret%d" % r], S.sent, pid, rid, m_short)
+            sent += _engines(m_short)
     g.wait_ge(S.sent, sent)
 
     n_sync = 0
@@ -347,7 +356,7 @@ def rank_program(g, core, T, topo):
     for e in reversed(P["pieces"][r]["mine"]):
         s = send[(r, e)]
         c0, c1 = s["a"], s["a"] + s["cnt"]
-        wait(yq, "ret%d" % e, _engines(topo.mask(T.cores[e], core)))
+        wait(yq, "ret%d" % e, _engines(short_mask(T.cores[e])))
         yq.dma_start(T.y[:, c0:c1], T.yr[:, c0:c1]).then_inc(S.st, 16)
         n_sync += 16
     wait(yq, "st", n_sync)

from concourse.bass import DstId, RemoteDMATransfer
from concourse.mybir import dt, AluOpType, ActivationFunctionType

NC = 512
TW = 128
G = 4
SLOT = (G + 1) * TW
NSLOT = 3
CONST = 0.029
BANK = 512
HC = 1024
RUNS = 6
NEXP = 6
GO = ((0, 2), (1, 2), (2, 1), (2, 3), (3, 4), (3, 5), (4, 0), (5, 4))

SCRATCH = {
    "xt": ("sbuf", [128, 4 * NC], "bfloat16"),
    "w1t": ("sbuf", [128, 4 * G * TW], "bfloat16"),
    "w2t": ("sbuf", [128, 4 * TW], "bfloat16"),
    "xq": ("sbuf", [128, NC], "float8_e4m3fn_x4"),
    "xs": ("sbuf", [128, NC], "uint8"),
    "rq": ("sbuf", [128, NC], "float8_e4m3fn_x4"),
    "rs": ("sbuf", [128, NC], "uint8"),
    "wq": ("sbuf", [128, NSLOT * SLOT], "float8_e4m3fn_x4"),
    "ws": ("sbuf", [128, NSLOT * SLOT], "uint8"),
    "h": ("sbuf", [128, 4 * HC], "bfloat16"),
    "hq": ("sbuf", [128, HC], "float8_e4m3fn_x4"),
    "hs": ("sbuf", [128, HC], "uint8"),
    "px": ("sbuf", [128, NC], "float32"),
    "yl": ("sbuf", [128, NC], "float32"),
    "yr": ("sbuf", [128, NC], "float32"),
    "ps": ("psum", [128, 8 * BANK], "float32"),
}
SEMAPHORES = (["ld_w1", "ld_w2", "q_w1", "q_w2", "ms", "sent", "st", "st2", "tok0", "tok1"]
              + ["%s%d" % (p, k) for p in ("ld_x", "q_x") for k in range(4)]
              + ["%s%d" % (p, k) for p in ("wa", "wb", "ret") for k in range(NEXP)] + ["zb%d" % b for b in range(8)]
              + ["%s%d" % (p, k) for p in ("a", "hq", "pc") for k in range(RUNS)])


def _blocks(a, b):
    return set(range(a // TW, (b - 1) // TW + 1))


def _plan(T):
    cnt = T.tables["CNT"]
    n = len(T.cores)
    off = [[sum(row[:e]) for e in range(n + 1)] for row in cnt]
    go = set(GO)
    for j, e in go:
        assert j != e and cnt[j][e]
    src = [[j for j in range(n) if j != e and cnt[j][e] and (j, e) not in go] for e in range(n)]
    total = [sum(cnt[j][e] for j in src[e]) for e in range(n)]
    urgent = [set() for _ in range(n)]
    for e in range(n):
        for j in src[e]:
            urgent[j] |= _blocks(off[j][e], off[j][e + 1])
    send = {}
    groups = []
    for e in range(n):
        order = sorted(src[e], key=lambda j: -cnt[j][e])
        pad = max(0, TW - total[e]) if order else 0
        if pad:
            fit = [j for j in order if off[j][e + 1] + pad <= NC]
            k = min(fit, key=lambda j: len(_blocks(off[j][e], off[j][e + 1] + pad) - urgent[j]))
            order.remove(k)
            order.append(k)
            urgent[k] |= _blocks(off[k][e], off[k][e + 1] + pad)
        pos = 0
        for j in order:
            w = cnt[j][e] + (pad if j == order[-1] else 0)
            send[(j, e)] = {"a": off[j][e], "w": w, "cnt": cnt[j][e], "pos": pos, "grp": 0}
            pos += w
        cut = None
        for k in range(1, len(order)):
            left = sum(cnt[j][e] for j in order[:k])
            if left >= TW and total[e] - left >= TW:
                cut = k
        if cut is None:
            groups.append([order] if order else [])
        else:
            groups.append([order[:cut], order[cut:]])
            for j in order[cut:]:
                send[(j, e)]["grp"] = 1
    pieces = []
    for j in range(n):
        mine = sorted([e for e in range(n) if (j, e) in send], key=lambda e: -total[e])
        first, rest = [], []
        for want, out in ((True, first), (False, rest)):
            k = 0
            while k < NC // TW:
                if (k in urgent[j]) == want:
                    k0 = k
                    while k < NC // TW and (k in urgent[j]) == want:
                        k += 1
                    out.append((k0 * TW, k * TW))
                else:
                    k += 1

        def rank_of_piece(p):
            return min(i for i, e in enumerate(mine)
                       if send[(j, e)]["a"] < p[1] and p[0] < send[(j, e)]["a"] + send[(j, e)]["w"])
        first.sort(key=rank_of_piece)
        pieces.append({"first": first, "rest": rest, "mine": mine})
    return {"cnt": cnt, "off": off, "send": send, "groups": groups, "pieces": pieces, "total": total}


def _engines(mask):
    return bin(mask).count("1")


def _slot(j, e):
    if e == j:
        return 0
    return 1 + sorted(e2 for (j2, e2) in GO if j2 == j).index(e)


def rank_program(g, core, T, topo):
    r = T.rank_of(core)
    if r is None:
        return
    P = _plan(T)
    S = T.sem
    tq, vq, sq, yq = g.tensor, g.vector, g.scalar, g.sync
    u8 = dt.uint8
    cnt, off, send = P["cnt"], P["off"], P["send"]
    n_ranks = len(T.cores)
    pcs = P["pieces"][r]["first"] + P["pieces"][r]["rest"]
    n_first = len(P["pieces"][r]["first"])

    seen = {}

    def wait(q, name, val):
        k = (q is tq, q is vq, q is sq, q is yq, name)
        if seen.get(k, 0) < val:
            seen[k] = val
            q.wait_ge(S[name], val)

    def wait_x(q, a, b):
        for k, p in enumerate(pcs):
            if p[0] < b and a < p[1]:
                wait(q, "q_x%d" % k, 1)

    def short_mask(c):
        mm = None
        for d in T.cores:
            if d != c:
                mm = topo.mask(c, d) if mm is None else mm & topo.mask(c, d)
        return mm

    def w_way(e):
        ways = []
        takers = [j for (j, e2) in GO if e2 == e]
        for ch in sorted(set(topo.chip(T.cores[j]) for j in takers)):
            tk = sorted(j for j in takers if topo.chip(T.cores[j]) == ch)
            mm = topo.mask(T.cores[e], T.cores[tk[0]])
            for k in tk:
                assert topo.may_write(T.cores[e], T.cores[k])
                mm &= topo.mask(T.cores[e], T.cores[k])
            ways.append((tk, mm))
        return ways

    def own_run(e):
        c = cnt[r][e]
        n = max(c, TW)
        a = min(off[r][e], NC - n)
        return {"e": e, "cnt": c, "n": n, "a": a, "lo": off[r][e] - a, "oc": off[r][e], "afar": False}

    diag = [own_run(r)] if cnt[r][r] else []
    here = topo.chip(core)
    wruns = [own_run(e) for e in sorted((e for (j, e) in GO if j == r),
                                        key=lambda e: (topo.chip(T.cores[e]) != here, -cnt[r][e]))]
    truns = []
    for gi, grp in enumerate(P["groups"][r]):
        p0 = send[(grp[0], r)]["pos"]
        truns.append({"e": r, "cnt": sum(cnt[j][r] for j in grp), "n": sum(send[(j, r)]["w"] for j in grp), "a": p0,
                      "lo": 0, "oc": p0, "afar": True, "grp": gi, "from": grp,
                      "tokn": sum(2 * _engines(short_mask(T.cores[j])) for j in grp)})
    assert sum(s["n"] for s in diag + truns + wruns) >= NC

    hb = 0
    fills = 0
    for k, run in enumerate(diag + truns + wruns):
        run["id"] = k
        run["hb"] = hb
        hb += run["n"]
        if run["cnt"] < run["n"]:
            vq.memset(T.h[:, 4 * (run["hb"] + run["cnt"]):4 * hb], 0.0).then_inc(S.ms, 1)
            fills += 1
    assert hb <= HC

    def load_x(k):
        a, b = pcs[k]
        yq.dma_start(T.xt[:, 4 * a:4 * b], T.x[:, 4 * a:4 * b]).then_inc(S["ld_x%d" % k], 16)

    def pack_x(k):
        a, b = pcs[k]
        wait(vq, "ld_x%d" % k, 16)
        vq.quantize_mx(T.xq[:, a:b], T.xs[:, a:b], T.xt[:, 4 * a:4 * b]).then_inc(S["q_x%d" % k], 1)

    for k in range(n_first):
        load_x(k)
    yq.dma_start(T.w1t[:], T.w1[:]).then_inc(S.ld_w1, 16)
    yq.dma_start(T.w2t[:], T.w2[:]).then_inc(S.ld_w2, 16)
    for k in range(n_first, len(pcs)):
        load_x(k)

    w2b = G * TW
    for k in range(n_first):
        pack_x(k)
    wait(vq, "ld_w1", 16)
    vq.quantize_mx(T.wq[:, 0:w2b], T.ws[:, 0:w2b], T.w1t[:]).then_inc(S.q_w1, 1)
    wait(vq, "ld_w2", 16)
    vq.quantize_mx(T.wq[:, w2b:SLOT], T.ws[:, w2b:SLOT], T.w2t[:]).then_inc(S.q_w2, 1)
    for k in range(n_first, len(pcs)):
        pack_x(k)
    if fills:
        wait(vq, "ms", fills)

    sent = 0
    m_short = short_mask(core)
    for e in P["pieces"][r]["mine"]:
        s = send[(r, e)]
        dst = T.cores[e]
        assert topo.may_write(core, dst)
        rid, pid, _ = topo.addr(dst)
        a, w, p = s["a"], s["w"], s["pos"]
        wait_x(g, a, a + w)
        tok = S["tok%d" % s["grp"]]
        g.remote_dma(T.rq[:, p:p + w].bitcast(u8), T.xq[:, a:a + w].bitcast(u8), tok, S.sent, pid, rid, m_short)
        g.remote_dma(T.rs[:, p:p + w], T.xs[:, a:a + w], tok, S.sent, pid, rid, m_short)
        sent += 2 * _engines(m_short)

    ways = w_way(r)
    for c0, c1, name, ready in ((0, w2b, "wa", "q_w1"), (w2b, SLOT, "wb", "q_w2")):
        if ways:
            wait(g, ready, 1)
        for takers, m in ways:
            ids = []
            for k in takers:
                rid, pid, _ = topo.addr(T.cores[k])
                ids.append(DstId(rid=rid, pnc=pid))
            bases = [_slot(k, r) * SLOT for k in takers]
            g.remote_dma_fused([RemoteDMATransfer(dst_ids=ids, dma_engine_mask=m, remote_sem=S["%s%d" % (name, r)],
                                                  srcs=[T.wq[:, c0:c1].bitcast(u8)],
                                                  dsts=[T.wq[:, b + c0:b + c1].bitcast(u8) for b in bases])],
                               local_sem=S.sent)
            g.remote_dma_fused([RemoteDMATransfer(dst_ids=ids, dma_engine_mask=m, remote_sem=S["%s%d" % (name, r)],
                                                  srcs=[T.ws[:, c0:c1]],
                                                  dsts=[T.ws[:, b + c0:b + c1] for b in bases])], local_sem=S.sent)
            sent += 2 * _engines(m)

    def w_arrival(e, name):
        for tk, mm in w_way(e):
            if r in tk:
                return "%s%d" % (name, e), 2 * _engines(mm)

    written = [0] * 8
    release = [None] * 8
    jobs = [0]

    def layer1(run):
        run["set"] = 4 * (jobs[0] % 2)
        jobs[0] += 1
        sem_a = "a%d" % run["id"]
        e, n, a = run["e"], run["n"], run["a"]
        if run["afar"]:
            wait(tq, "tok%d" % run["grp"], run["tokn"])
            rhs, rhs_s = T.rq[:, a:a + n], T.rs[:, a:a + n]
        else:
            wait_x(tq, a, a + n)
            rhs, rhs_s = T.xq[:, a:a + n], T.xs[:, a:a + n]
        if e == r:
            wait(tq, "q_w1", 1)
        else:
            wait(tq, *w_arrival(e, "wa"))
        wb = _slot(r, e) * SLOT
        lo = run["lo"]
        for i in range(G):
            b = run["set"] + i
            if release[b]:
                wait(tq, *release[b])
            tq.matmul_mx(T.ps[:, b * BANK:b * BANK + n], T.wq[:, wb + i * TW:wb + (i + 1) * TW],
                         T.ws[:, wb + i * TW:wb + (i + 1) * TW], rhs, rhs_s, True, True).then_inc(S["zb%d" % b], 1)
            written[b] += 1
            z = T.ps[:, b * BANK + lo:b * BANK + lo + run["cnt"]]
            out = T.h[:, 4 * run["hb"] + i:4 * (run["hb"] + run["cnt"]):4]
            if i % 2 == 0:
                wait(sq, "zb%d" % b, written[b])
                sq.activation(out, z, ActivationFunctionType.Relu, scale=CONST).then_inc(S[sem_a], 1)
            else:
                wait(vq, "zb%d" % b, written[b])
                vq.tensor_scalar(out, z, 0.0, CONST, AluOpType.max, AluOpType.mult).then_inc(S[sem_a], 1)
            release[b] = (sem_a, G)
        c0, c1 = run["hb"], run["hb"] + n
        wait(vq, sem_a, G)
        vq.quantize_mx(T.hq[:, c0:c1], T.hs[:, c0:c1], T.h[:, 4 * c0:4 * c1]).then_inc(S["hq%d" % run["id"]], 1)

    def layer2(run, out, on_vector):
        b = run["set"]
        e, n = run["e"], run["n"]
        c0, c1 = run["hb"], run["hb"] + n
        wait(tq, "hq%d" % run["id"], 1)
        if e == r:
            wait(tq, "q_w2", 1)
        else:
            wait(tq, *w_arrival(e, "wb"))
        wait(tq, *release[b])
        wb = _slot(r, e) * SLOT + G * TW
        tq.matmul_mx(T.ps[:, b * BANK:b * BANK + n], T.wq[:, wb:wb + TW], T.ws[:, wb:wb + TW],
                     T.hq[:, c0:c1], T.hs[:, c0:c1], True, True).then_inc(S["zb%d" % b], 1)
        written[b] += 1
        o, p = out[:, run["oc"]:run["oc"] + run["cnt"]], T.ps[:, b * BANK:b * BANK + run["cnt"]]
        if on_vector:
            wait(vq, "zb%d" % b, written[b])
            vq.tensor_copy(o, p).then_inc(S["pc%d" % run["id"]], 1)
        else:
            wait(sq, "zb%d" % b, written[b])
            sq.activation(o, p, ActivationFunctionType.Copy).then_inc(S["pc%d" % run["id"]], 1)
        release[b] = ("pc%d" % run["id"], 1)

    def batch(runs, out):
        for k in range(0, len(runs), 2):
            for run in runs[k:k + 2]:
                layer1(run)
            for j, run in enumerate(runs[k:k + 2]):
                layer2(run, out, j == 1)

    batch(diag, T.yl)
    batch(truns, T.px)
    batch(wruns, T.yl)

    for run in truns:
        wait(g, "pc%d" % run["id"], 1)
        for j in run["from"]:
            s = send[(j, r)]
            dst = T.cores[j]
            assert topo.may_write(core, dst)
            rid, pid, _ = topo.addr(dst)
            g.remote_dma(T.yr[:, s["a"]:s["a"] + s["cnt"]], T.px[:, s["pos"]:s["pos"] + s["cnt"]],
                         S["ret%d" % r], S.sent, pid, rid, m_short)
            sent += _engines(m_short)
    g.wait_ge(S.sent, sent)

    n_sync = 0
    n_scal = 0
    for run in diag:
        c0, c1 = run["oc"], run["oc"] + run["cnt"]
        wait(yq, "pc%d" % run["id"], 1)
        yq.dma_start(T.y[:, c0:c1], T.yl[:, c0:c1]).then_inc(S.st, 16)
        n_sync += 16
    for run in wruns:
        c0, c1 = run["oc"], run["oc"] + run["cnt"]
        wait(sq, "pc%d" % run["id"], 1)
        sq.dma_start(T.y[:, c0:c1], T.yl[:, c0:c1]).then_inc(S.st2, 16)
        n_scal += 16
    for e in reversed(P["pieces"][r]["mine"]):
        s = send[(r, e)]
        c0, c1 = s["a"], s["a"] + s["cnt"]
        wait(yq, "ret%d" % e, _engines(short_mask(T.cores[e])))
        yq.dma_start(T.y[:, c0:c1], T.yr[:, c0:c1]).then_inc(S.st, 16)
        n_sync += 16
    wait(yq, "st", n_sync)
    if n_scal:
        wait(sq, "st2", n_scal)
    assert n_ranks == NEXP
